import numpy as np
import ml_dtypes


def mxq(x, axis, fmt="e4m3"):
    dtype, down = {"e4m3": (ml_dtypes.float8_e4m3fn, 7), "e5m2": (ml_dtypes.float8_e5m2, 14)}[fmt]
    v = np.moveaxis(np.asarray(x, np.float32).astype(ml_dtypes.bfloat16).astype(np.float64), axis, -1)
    blocks = v.reshape(v.shape[:-1] + (-1, 32))
    amax = np.abs(blocks).max(-1, keepdims=True)
    byte = np.maximum(np.where(amax > 0, np.frexp(amax)[1] - 1 + 127, 0) - down, 1)
    scale = np.exp2(byte - 127.0)
    codes = (blocks / scale).astype(np.float32).astype(dtype).astype(np.float64)
    return np.moveaxis((codes * scale).reshape(v.shape), -1, axis)


WIDE = False


def mx_kscale(k):
    if not WIDE:
        return np.ones(k)
    levels = np.array([10, -10, 5, -5, 0])
    if k % 512:
        return np.exp2(np.random.permutation(np.resize(levels, k // 32))).repeat(32)
    a = np.empty((k // 512, 16))
    for p in range(k // 512):
        a[p, :8] = np.random.permutation(np.resize(levels, 8))
        for g in range(8):
            far = levels[np.abs(levels - a[p, g]) >= 10]
            a[p, g + 8] = far[np.random.randint(len(far))]
    return np.exp2(a.ravel()).repeat(32)


BF16 = ml_dtypes.bfloat16


def bf(x):
    return np.asarray(x, np.float32).astype(BF16)


def f64(x):
    return np.asarray(x).astype(np.float64)


E2M1 = np.array([0.0, 0.5, 1.0, 1.5, 2.0, 3.0, 4.0, 6.0, -0.0, -0.5, -1.0, -1.5, -2.0, -3.0, -4.0, -6.0])


def pack_weight(w, fmt):
    k, n = w.shape
    w = f64(bf(w)).reshape(k // 32, 32, n)
    amax = np.abs(w).max(1)
    if fmt == "e4m3":
        byte = np.frexp(amax)[1] - 1 + 127 - 7
    else:
        mant, ex = np.frexp(amax / 6.0)
        byte = np.where(mant > 0.5, ex, ex - 1) + 127
    byte = np.clip(np.where(amax > 0, byte, 1), 1, 254)
    scaled = (w * np.exp2(127.0 - byte)[:, None, :]).reshape(k, n).astype(np.float32)
    by_word = np.ascontiguousarray(scaled.reshape(k // 512, 128, 4, n).transpose(0, 1, 3, 2))
    if fmt == "e4m3":
        words = by_word.astype(ml_dtypes.float8_e4m3fn).view(np.uint8)
    else:
        c = by_word.astype(ml_dtypes.float4_e2m1fn).view(np.uint8) & 0xF
        words = c[..., 0::2] | (c[..., 1::2] << 4)
    return np.ascontiguousarray(words), np.ascontiguousarray(byte.astype(np.uint8).reshape(k // 512, 16, n))


def unpack_weight(words, scales, fmt):
    g, p, n, _ = words.shape
    if fmt == "e4m3":
        vals = np.ascontiguousarray(words).view(ml_dtypes.float8_e4m3fn).astype(np.float64)
    else:
        nib = np.empty((g, p, n, 4), np.uint8)
        nib[..., 0::2] = words & 0xF
        nib[..., 1::2] = words >> 4
        vals = E2M1[nib]
    vals = vals * np.repeat(np.exp2(scales.astype(np.float64) - 127.0), 8, axis=1)[..., None]
    return vals.transpose(0, 1, 3, 2).reshape(g * 512, n)

def planes(Y):
    n, m = Y.shape
    b = f64(bf(Y)).reshape(n // 32, 32, m)
    amax = np.abs(b).max(1)
    byte = np.clip(np.where(amax > 0, np.frexp(amax)[1] - 1 + 127 - 7, 1), 1, 254)
    codes = (b * np.exp2(127.0 - byte)[:, None, :]).reshape(n, m).astype(np.float32).astype(ml_dtypes.float8_e4m3fn).view(np.uint8)
    words = codes.reshape(n // 512, 128, 4, m).transpose(0, 1, 3, 2)
    return np.ascontiguousarray(words), np.ascontiguousarray(byte.astype(np.uint8).reshape(n // 512, 16, m))


T, D = 1024, 1024


def setup_inputs():
    s = mx_kscale(D)
    t = mx_kscale(D)
    inv = 1.0 / np.sqrt(D)
    r = np.where(np.random.random((T, 1)) < 0.25, 0.001, 1.0)
    x = bf((0.5 + 1.5 * np.random.standard_normal((T, D))) * r)
    c = bf(np.random.standard_normal((T, D)) * s)
    wsc_words, wsc_scales = pack_weight(np.random.standard_normal((D, D)) * 0.5 * inv / s[:, None] * t, "e4m3")
    bsc = bf((1.0 + 0.1 * np.random.standard_normal(D)) * t)
    wsh_words, wsh_scales = pack_weight(np.random.standard_normal((D, D)) * 0.5 * inv / s[:, None] * t, "e4m3")
    wg_words, wg_scales = pack_weight(np.random.standard_normal((D, D)) * inv / s[:, None], "e4m3")
    w_words, w_scales = pack_weight(np.random.standard_normal((D, D)) * inv / t[:, None], "e4m3")
    return {
        "x": x,
        "c": c,
        "wsc_words": wsc_words,
        "wsc_scales": wsc_scales,
        "bsc": bsc,
        "wsh_words": wsh_words,
        "wsh_scales": wsh_scales,
        "wg_words": wg_words,
        "wg_scales": wg_scales,
        "w_words": w_words,
        "w_scales": w_scales,
    }


def _normalize(x):
    mean = np.mean(x, axis=-1, keepdims=True)
    centered = x - mean
    var = np.mean(centered * centered, axis=-1, keepdims=True)
    return centered / np.sqrt(var + 1e-6)


def core(x, c, wsc_words, wsc_scales, bsc, wsh_words, wsh_scales, wg_words, wg_scales, w_words, w_scales):
    x = f64(x)
    n = _normalize(x)
    cq = mxq(f64(c), 1, "e4m3")
    scale = (cq @ unpack_weight(wsc_words, wsc_scales, "e4m3")) + f64(bsc)
    shift = cq @ unpack_weight(wsh_words, wsh_scales, "e4m3")
    gate = cq @ unpack_weight(wg_words, wg_scales, "e4m3")
    y = n * scale + shift
    f = mxq(y, 1, "e4m3") @ unpack_weight(w_words, w_scales, "e4m3")
    return x + gate * f


def reference(x, c, wsc_words, wsc_scales, bsc, wsh_words, wsh_scales, wg_words, wg_scales, w_words, w_scales):
    R_out = core(x, c, wsc_words, wsc_scales, bsc, wsh_words, wsh_scales, wg_words, wg_scales, w_words, w_scales)
    words, scales = planes(R_out.T)
    return R_out, words, scales

@@ -1,0 +1,333 @@
+from contextlib import ExitStack
+
+import concourse.mybir as mybir
+from concourse.masks import make_identity
+
+T, D = 1024, 1024
+FLOPS = 4 * 2 * T * D * D
+
+F32 = mybir.dt.float32
+BF16 = mybir.dt.bfloat16
+I32 = mybir.dt.int32
+U32 = mybir.dt.uint32
+U8 = mybir.dt.uint8
+FP8X4 = mybir.dt.float8_e4m3fn_x4
+ALU = mybir.AluOpType
+ACT = mybir.ActivationFunctionType
+
+P = 128
+GROUPS = 2
+HALF = 512
+TILES = T // P
+EPS = 1e-6
+
+
+def tile_diffusionforcingpertokenadalnzero_x2_kernel(
+    tc, x, c, wsc_words, wsc_scales, bsc, wsh_words, wsh_scales, wg_words, wg_scales, w_words, w_scales,
+    out_0, out_1, out_2,
+):
+    nc = tc.nc
+    with ExitStack() as ctx:
+        keep = ctx.enter_context(tc.tile_pool(name="keep", bufs=1))
+        two = ctx.enter_context(tc.tile_pool(name="two", bufs=2))
+        three = ctx.enter_context(tc.tile_pool(name="three", bufs=3))
+        four = ctx.enter_context(tc.tile_pool(name="four", bufs=4))
+        psum = ctx.enter_context(tc.psum_pool(name="psum", bufs=1))
+        ctx.enter_context(tc.manual_schedule())
+
+        def bank(tag):
+            return psum.tile([P, HALF], F32, name=tag)
+
+        ident = keep.tile([P, P], F32, name="ident")
+        ones = keep.tile([P, P], BF16, name="ones")
+        bias_row = keep.tile([P, D], BF16, name="bias_row")
+        bias_all = keep.tile([P, D], BF16, name="bias_all")
+        minus_half = keep.tile([P, 1], F32, name="minus_half")
+        warm = keep.tile([P, 1], F32, name="warm")
+        x_sb = [keep.tile([P, D], BF16, name="x%d" % i) for i in range(TILES)]
+        c_sb = [keep.tile([P, D], BF16, name="c%d" % i) for i in range(TILES)]
+        names = ("wsc", "wsh", "wg", "w")
+        hbm_words = dict(zip(names, (wsc_words, wsh_words, wg_words, w_words)))
+        hbm_scales = dict(zip(names, (wsc_scales, wsh_scales, wg_scales, w_scales)))
+        first_row = dict(zip(names, (0, 8, 0, 8)))
+        words = {}
+        scales = {}
+        for n in names:
+            words[n] = [keep.tile([P, GROUPS, HALF], U32, name="%s_words%d" % (n, h), align_bytes=64) for h in range(2)]
+            scales[n] = keep.tile([P, D], U8, name="%s_scales" % n, align_bytes=64)
+        out_words = keep.tile([P, GROUPS, T], U32, name="out_words", align_bytes=64)
+        out_scales = keep.tile([P, GROUPS, T], U8, name="out_scales", align_bytes=64)
+
+        def load_rows(dst, src, i):
+            nc.sync.dma_start(out=dst[i][:], in_=src[P * i : P * (i + 1), :])
+
+        def load_scales(n):
+            for q in range(4):
+                r = 32 * q + first_row[n]
+                nc.sync.dma_start(
+                    out=scales[n][:].bitcast(I32)[r : r + 8, :],
+                    in_=hbm_scales[n][:, 4 * q : 4 * q + 4, :].bitcast(I32),
+                )
+
+        def load_words(n, h):
+            src = hbm_words[n].rearrange("g p n t -> p g (n t)")[:, :, 4 * HALF * h : 4 * HALF * (h + 1)]
+            nc.sync.dma_start(out=words[n][h][:].bitcast(I32), in_=src.bitcast(I32))
+
+        nc.vector.memset(bias_row[:], 0.0)
+        nc.vector.memset(scales["wsc"][:].bitcast(I32), 0)
+        nc.vector.memset(minus_half[:], -0.5)
+        nc.vector.memset(ones[:], 1.0)
+        for n in names[1:]:
+            nc.vector.memset(scales[n][:].bitcast(I32), 0)
+        make_identity(nc, ident[:])
+        nc.scalar.activation(out=warm[:], in_=minus_half[:], func=ACT.Square)
+
+        load_rows(c_sb, c, 0)
+        nc.sync.dma_start(out=bias_row[0:1, :], in_=bsc.rearrange("(o n) -> o n", o=1))
+        load_scales("wsc")
+        load_words("wsc", 0)
+        load_rows(x_sb, x, 0)
+        load_words("wsc", 1)
+        load_rows(c_sb, c, 1)
+        load_scales("wsh")
+        load_words("wsh", 0)
+        load_words("wsh", 1)
+        load_rows(c_sb, c, 2)
+        load_rows(x_sb, x, 1)
+        load_scales("wg")
+        load_words("wg", 0)
+        load_words("wg", 1)
+        load_scales("w")
+        load_words("w", 0)
+        load_words("w", 1)
+        for i in range(3, TILES + 1):
+            if i < TILES:
+                load_rows(c_sb, c, i)
+            load_rows(x_sb, x, i - 1)
+
+        st = {}
+
+        def turn(key, tag, src_words):
+            b = bank(tag)
+            for g in range(GROUPS):
+                for u in range(2):
+                    j = 2 * g + u
+                    nc.tensor.transpose(b[:, P * j : P * (j + 1)], src_words(g, u), ident[:])
+            st[key] = b
+
+        def turn_c(i):
+            wv = c_sb[i][:].bitcast(F32)
+            turn(("cT", i), "turn_c", lambda g, u: wv[:, 256 * g + u : 256 * (g + 1) : 2])
+
+        def turn_sorted(key, tag, tile):
+            wv = tile[:].bitcast(F32)
+            turn(key, tag, lambda g, u: wv[:, 256 * u + P * g : 256 * u + P * (g + 1)])
+
+        def unload_turned(key, name, groups=(0, GROUPS)):
+            if (name, key) not in st:
+                st[(name, key)] = two.tile([P, GROUPS, P, 4], BF16, name=name, align_bytes=64)
+            dst = st[(name, key)]
+            g0, g1 = groups
+            nc.scalar.copy(
+                out=dst[:].rearrange("p g r t -> p (g r t)").bitcast(F32).rearrange("p (g r u) -> p g r u", g=GROUPS, u=2)[:, g0:g1],
+                in_=st[key][:].rearrange("p (g u r) -> p g r u", g=GROUPS, u=2)[:, g0:g1],
+            )
+
+        def quantise(key, name, pool):
+            src = st[(name, key)]
+            codes = pool.tile([P, GROUPS * P], U32, name=name + "_codes", align_bytes=64)
+            plane = pool.tile([P, GROUPS * P], U8, name=name + "_plane", align_bytes=64)
+            nc.vector.quantize_mx(
+                out=codes[:].bitcast(FP8X4), scales=plane[:], in_=src[:].rearrange("p g r t -> p (g r t)")
+            )
+            st[(name + "q", key[1])] = (codes, plane)
+
+        def product(key, n, operand, tags):
+            codes, plane = operand
+            banks = []
+            for h in range(2):
+                b = bank(tags[h])
+                for g in range(GROUPS):
+                    k = first_row[n] + 4 * g
+                    nc.tensor.matmul_mx(
+                        out=b[:],
+                        lhsT=codes[:, P * g : P * (g + 1)].bitcast(FP8X4),
+                        lhsT_scale=plane[:, P * g : P * (g + 1)],
+                        rhs=words[n][h][:, g, :].bitcast(FP8X4),
+                        rhs_scale=scales[n][k:P, HALF * h : HALF * (h + 1)],
+                        start=(g == 0),
+                        stop=(g == GROUPS - 1),
+                    )
+                banks.append(b)
+            st[key] = banks
+
+        def row_mean(i):
+            stats = three.tile([P, 8], F32, name="stats")
+            junk = two.tile([P, D], BF16, name="junk")
+            nc.scalar.activation(out=junk[:], in_=x_sb[i][:], func=ACT.Copy, scale=-1.0 / D, accum_out=stats[:, 0:1])
+            st[("stats", i)] = stats
+
+        def row_rstd(i):
+            stats = st[("stats", i)]
+            junk = two.tile([P, D], BF16, name="junk")
+            nc.scalar.activation(
+                out=junk[:], in_=x_sb[i][:], func=ACT.Square, bias=stats[:, 0:1], accum_out=stats[:, 1:2]
+            )
+            var = three.tile([P, 1], F32, name="var")
+            rstd = three.tile([P, 1], F32, name="rstd")
+            nc.gpsimd.tensor_scalar(
+                out=var[:], in0=stats[:, 1:2], scalar1=1.0 / D, scalar2=EPS, op0=ALU.mult, op1=ALU.add
+            )
+            nc.gpsimd.tensor_tensor(out=rstd[:], in0=var[:], in1=minus_half[:], op=ALU.pow)
+            st[("rstd", i)] = rstd
+
+        def add_bias(i):
+            a = two.tile([P, D], F32, name="gain")
+            for h in range(2):
+                cols = slice(HALF * h, HALF * (h + 1))
+                nc.vector.tensor_tensor(out=a[:, cols], in0=st[("S", i)][h][:], in1=bias_all[:, cols], op=ALU.add)
+            st[("gain", i)] = a
+
+        def centre_times_gain(i):
+            t = two.tile([P, D], F32, name="scaled")
+            nc.vector.scalar_tensor_tensor(
+                out=t[:], in0=x_sb[i][:], scalar=st[("stats", i)][:, 0:1], in1=st[("gain", i)][:],
+                op0=ALU.add, op1=ALU.mult,
+            )
+            st[("scaled", i)] = t
+
+        def make_y(i):
+            y = two.tile([P, 2, GROUPS, P, 2], BF16, name="y")
+            t = st[("scaled", i)]
+            for g in range(GROUPS):
+                tv = t[:, HALF * g : HALF * (g + 1)].rearrange("p (m u e) -> p u m e", u=2, e=2)
+                hv = st[("H", i)][g][:].rearrange("p (m u e) -> p u m e", u=2, e=2)
+                for u in range(2):
+                    nc.vector.scalar_tensor_tensor(
+                        out=y[:, u, g], in0=tv[:, u], scalar=st[("rstd", i)][:], in1=hv[:, u],
+                        op0=ALU.mult, op1=ALU.add,
+                    )
+            st[("y", i)] = y[:].rearrange("p u g m e -> p (u g m e)")
+
+        def unload_gate(i):
+            gate = two.tile([P, D], F32, name="gate")
+            for h in range(2):
+                nc.scalar.copy(out=gate[:, HALF * h : HALF * (h + 1)], in_=st[("G", i)][h][:])
+            st[("gate", i)] = gate
+
+        def gate_times_f(i):
+            gated = two.tile([P, D], F32, name="gated")
+            for h in range(2):
+                cols = slice(HALF * h, HALF * (h + 1))
+                nc.vector.tensor_tensor(out=gated[:, cols], in0=st[("F", i)][h][:], in1=st[("gate", i)][:, cols], op=ALU.mult)
+            st[("gated", i)] = gated
+
+        def add_residual(i, parts):
+            res = three.tile([P, D], F32, name="result")
+            for h in range(parts):
+                cols = slice(D // parts * h, D // parts * (h + 1))
+                nc.vector.tensor_tensor(out=res[:, cols], in0=st[("gated", i)][:, cols], in1=x_sb[i][:, cols], op=ALU.add)
+                nc.sync.dma_start(out=out_0[P * i : P * (i + 1), cols], in_=res[:, cols])
+            st[("result", i)] = res
+
+        def round_result(i, groups=(0, GROUPS)):
+            if ("rounded", i) not in st:
+                st[("rounded", i)] = two.tile([P, D], BF16, name="rounded")
+            g0, g1 = groups
+            nc.scalar.copy(
+                out=st[("rounded", i)][:].rearrange("p (u m e) -> p u m e", u=2, e=2)[:, :, P * g0 : P * g1],
+                in_=st[("result", i)][:].rearrange("p (m u e) -> p u m e", u=2, e=2)[:, :, P * g0 : P * g1],
+            )
+
+        def quantise_result(i, groups=(0, GROUPS)):
+            src = st[("og", ("oT", i))]
+            cols = slice(P * i, P * (i + 1))
+            for g in range(*groups):
+                nc.vector.quantize_mx(
+                    out=out_words[:, g, cols].bitcast(FP8X4), scales=out_scales[:, g, cols],
+                    in_=src[:, g].rearrange("p r t -> p (r t)"),
+                )
+
+        def store_words(i0, i1):
+            dst = out_1.rearrange("g p m t -> p g (m t)")[:, :, 4 * P * i0 : 4 * P * i1]
+            nc.sync.dma_start(out=dst.bitcast(I32), in_=out_words[:, :, P * i0 : P * i1].bitcast(I32))
+
+        def store_scales(i0, i1, engines):
+            for q in range(4):
+                engines[q % len(engines)].dma_start(
+                    out=out_2[:, 4 * q : 4 * q + 4, P * i0 : P * i1].rearrange("g r m -> r g m").bitcast(I32),
+                    in_=out_scales[32 * q : 32 * q + 4, :, P * i0 : P * i1].bitcast(I32),
+                )
+
+        turn_c(0)
+        unload_turned(("cT", 0), "cg")
+        for h in range(2):
+            b = bank("f%d" % h)
+            nc.tensor.matmul(out=b[:], lhsT=ones[:], rhs=bias_row[:, HALF * h : HALF * (h + 1)], start=True, stop=True)
+            nc.vector.tensor_copy(out=bias_all[:, HALF * h : HALF * (h + 1)], in_=b[:])
+            if h == 0:
+                quantise(("cT", 0), "cg", four)
+        product(("S", 0), "wsc", st[("cgq", 0)], ("sg0", "sg1"))
+        row_mean(0)
+        turn_c(1)
+        unload_turned(("cT", 1), "cg")
+        row_rstd(0)
+
+        last = TILES - 1
+        for j in range(TILES + 1):
+            now, before = j <= last, 1 <= j
+            if j >= 2:
+                round_result(j - 2)
+            if now:
+                product(("H", j), "wsh", st[("cgq", j)], ("h0", "h1"))
+                add_bias(j)
+            if j + 1 <= last:
+                row_mean(j + 1)
+                quantise(("cT", j + 1), "cg", four)
+            if before:
+                product(("G", j - 1), "wg", st[("cgq", j - 1)], ("sg0", "sg1"))
+            if now:
+                centre_times_gain(j)
+            if before:
+                product(("F", j - 1), "w", st[("ygq", j - 1)], ("f0", "f1"))
+                unload_gate(j - 1)
+            if j >= 3:
+                quantise_result(j - 3)
+                if j % 2 == 0:
+                    store_words(j - 4, j - 2)
+            if now:
+                make_y(j)
+            if j + 1 <= last:
+                row_rstd(j + 1)
+            if j + 2 <= last:
+                turn_c(j + 2)
+            if now:
+                turn_sorted(("yT", j), "h0", st[("y", j)])
+            if j >= 2:
+                turn_sorted(("oT", j - 2), "turn_o", st[("rounded", j - 2)])
+            if now:
+                unload_turned(("yT", j), "yg")
+            if j + 2 <= last:
+                unload_turned(("cT", j + 2), "cg")
+            if j >= 2:
+                unload_turned(("oT", j - 2), "og")
+            if before:
+                gate_times_f(j - 1)
+            if now:
+                quantise(("yT", j), "yg", two)
+            if before:
+                add_residual(j - 1, 2 if j - 1 == last else 1)
+            if j + 1 <= last:
+                product(("S", j + 1), "wsc", st[("cgq", j + 1)], ("sg0", "sg1"))
+
+        quantise_result(last - 1)
+        store_words(last - 1, last)
+        store_scales(0, last, (nc.sync,))
+        for g in range(GROUPS):
+            round_result(last, (g, g + 1))
+        turn_sorted(("oT", last), "turn_c", st[("rounded", last)])
+        for g in range(GROUPS):
+            unload_turned(("oT", last), "og", (g, g + 1))
+            quantise_result(last, (g, g + 1))
+        store_words(last, TILES)
+        store_scales(last, TILES, (nc.scalar, nc.sync))

@@ -42,7 +42,6 @@ def tile_diffusionforcingpertokenadalnzero_x2_kernel(
         ones = keep.tile([P, P], BF16, name="ones")
         bias_row = keep.tile([P, D], BF16, name="bias_row")
         bias_all = keep.tile([P, D], BF16, name="bias_all")
-        minus_half = keep.tile([P, 1], F32, name="minus_half")
         warm = keep.tile([P, 1], F32, name="warm")
         x_sb = [keep.tile([P, D], BF16, name="x%d" % i) for i in range(TILES)]
         c_sb = [keep.tile([P, D], BF16, name="c%d" % i) for i in range(TILES)]
@@ -75,12 +74,11 @@ def tile_diffusionforcingpertokenadalnzero_x2_kernel(
 
         nc.vector.memset(bias_row[:], 0.0)
         nc.vector.memset(scales["wsc"][:].bitcast(I32), 0)
-        nc.vector.memset(minus_half[:], -0.5)
         nc.vector.memset(ones[:], 1.0)
         for n in names[1:]:
             nc.vector.memset(scales[n][:].bitcast(I32), 0)
         make_identity(nc, ident[:])
-        nc.scalar.activation(out=warm[:], in_=minus_half[:], func=ACT.Square)
+        nc.scalar.activation(out=warm[:], in_=ones[:, 0:1], func=ACT.Sqrt)
 
         load_rows(c_sb, c, 0)
         nc.sync.dma_start(out=bias_row[0:1, :], in_=bsc.rearrange("(o n) -> o n", o=1))
@@ -92,18 +90,20 @@ def tile_diffusionforcingpertokenadalnzero_x2_kernel(
         load_scales("wsh")
         load_words("wsh", 0)
         load_words("wsh", 1)
-        load_rows(c_sb, c, 2)
         load_rows(x_sb, x, 1)
+        load_rows(c_sb, c, 2)
+        load_rows(x_sb, x, 2)
+        load_rows(c_sb, c, 3)
         load_scales("wg")
         load_words("wg", 0)
         load_words("wg", 1)
         load_scales("w")
         load_words("w", 0)
         load_words("w", 1)
-        for i in range(3, TILES + 1):
+        for i in range(4, TILES + 1):
+            load_rows(x_sb, x, i - 1)
             if i < TILES:
                 load_rows(c_sb, c, i)
-            load_rows(x_sb, x, i - 1)
 
         st = {}
 
@@ -125,7 +125,7 @@ def tile_diffusionforcingpertokenadalnzero_x2_kernel(
 
         def unload_turned(key, name, groups=(0, GROUPS)):
             if (name, key) not in st:
-                st[(name, key)] = two.tile([P, GROUPS, P, 4], BF16, name=name, align_bytes=64)
+                st[(name, key)] = three.tile([P, GROUPS, P, 4], BF16, name=name, align_bytes=64)
             dst = st[(name, key)]
             g0, g1 = groups
             nc.scalar.copy(
@@ -162,77 +162,76 @@ def tile_diffusionforcingpertokenadalnzero_x2_kernel(
             st[key] = banks
 
         def row_mean(i):
-            stats = three.tile([P, 8], F32, name="stats")
+            stats = keep.tile([P, 8], F32, name="stats%d" % i)
             junk = two.tile([P, D], BF16, name="junk")
             nc.scalar.activation(out=junk[:], in_=x_sb[i][:], func=ACT.Copy, scale=-1.0 / D, accum_out=stats[:, 0:1])
             st[("stats", i)] = stats
 
-        def row_rstd(i):
+        def row_squares(i):
             stats = st[("stats", i)]
             junk = two.tile([P, D], BF16, name="junk")
             nc.scalar.activation(
                 out=junk[:], in_=x_sb[i][:], func=ACT.Square, bias=stats[:, 0:1], accum_out=stats[:, 1:2]
             )
-            var = three.tile([P, 1], F32, name="var")
-            rstd = three.tile([P, 1], F32, name="rstd")
-            nc.gpsimd.tensor_scalar(
-                out=var[:], in0=stats[:, 1:2], scalar1=1.0 / D, scalar2=EPS, op0=ALU.mult, op1=ALU.add
-            )
-            nc.gpsimd.tensor_tensor(out=rstd[:], in0=var[:], in1=minus_half[:], op=ALU.pow)
+
+        def row_std(i):
+            stats = st[("stats", i)]
+            nc.scalar.activation(out=stats[:, 2:3], in_=stats[:, 1:2], func=ACT.Sqrt, scale=1.0 / D, bias=EPS)
+
+        def row_rstd(i):
+            rstd = keep.tile([P, 1], F32, name="rstd%d" % i)
+            nc.vector.reciprocal(out=rstd[:], in_=st[("stats", i)][:, 2:3])
             st[("rstd", i)] = rstd
 
         def add_bias(i):
-            a = two.tile([P, D], F32, name="gain")
+            a = three.tile([P, D], F32, name="gain")
             for h in range(2):
                 cols = slice(HALF * h, HALF * (h + 1))
                 nc.vector.tensor_tensor(out=a[:, cols], in0=st[("S", i)][h][:], in1=bias_all[:, cols], op=ALU.add)
             st[("gain", i)] = a
 
         def centre_times_gain(i):
-            t = two.tile([P, D], F32, name="scaled")
+            a = st[("gain", i)]
             nc.vector.scalar_tensor_tensor(
-                out=t[:], in0=x_sb[i][:], scalar=st[("stats", i)][:, 0:1], in1=st[("gain", i)][:],
-                op0=ALU.add, op1=ALU.mult,
+                out=a[:], in0=x_sb[i][:], scalar=st[("stats", i)][:, 0:1], in1=a[:], op0=ALU.add, op1=ALU.mult
             )
-            st[("scaled", i)] = t
 
         def make_y(i):
-            y = two.tile([P, 2, GROUPS, P, 2], BF16, name="y")
-            t = st[("scaled", i)]
-            for g in range(GROUPS):
-                tv = t[:, HALF * g : HALF * (g + 1)].rearrange("p (m u e) -> p u m e", u=2, e=2)
-                hv = st[("H", i)][g][:].rearrange("p (m u e) -> p u m e", u=2, e=2)
-                for u in range(2):
-                    nc.vector.scalar_tensor_tensor(
-                        out=y[:, u, g], in0=tv[:, u], scalar=st[("rstd", i)][:], in1=hv[:, u],
-                        op0=ALU.mult, op1=ALU.add,
-                    )
-            st[("y", i)] = y[:].rearrange("p u g m e -> p (u g m e)")
-
-        def unload_gate(i):
-            gate = two.tile([P, D], F32, name="gate")
-            for h in range(2):
-                nc.scalar.copy(out=gate[:, HALF * h : HALF * (h + 1)], in_=st[("G", i)][h][:])
-            st[("gate", i)] = gate
-
-        def gate_times_f(i):
-            gated = two.tile([P, D], F32, name="gated")
+            y = three.tile([P, D], BF16, name="y")
             for h in range(2):
                 cols = slice(HALF * h, HALF * (h + 1))
-                nc.vector.tensor_tensor(out=gated[:, cols], in0=st[("F", i)][h][:], in1=st[("gate", i)][:, cols], op=ALU.mult)
-            st[("gated", i)] = gated
+                nc.vector.scalar_tensor_tensor(
+                    out=y[:, cols], in0=st[("gain", i)][:, cols], scalar=st[("rstd", i)][:], in1=st[("H", i)][h][:],
+                    op0=ALU.mult, op1=ALU.add,
+                )
+            st[("y", i)] = y
 
-        def add_residual(i, parts):
-            res = three.tile([P, D], F32, name="result")
+        def turn_y(i):
+            wv = st[("y", i)][:].bitcast(F32)
+            turn(("yT", i), "h0", lambda g, u: wv[:, 256 * g + u : 256 * (g + 1) : 2])
+
+        def unload_gate(i):
+            res = four.tile([P, D], F32, name="result")
+            for h in range(2):
+                nc.scalar.copy(out=res[:, HALF * h : HALF * (h + 1)], in_=st[("G", i)][h][:])
+            st[("result", i)] = res
+
+        def gate_times_f(i):
+            res = st[("result", i)]
+            for h in range(2):
+                cols = slice(HALF * h, HALF * (h + 1))
+                nc.vector.tensor_tensor(out=res[:, cols], in0=st[("F", i)][h][:], in1=res[:, cols], op=ALU.mult)
+
+        def add_residual(i, parts=1):
+            res = st[("result", i)]
             for h in range(parts):
                 cols = slice(D // parts * h, D // parts * (h + 1))
-                nc.vector.tensor_tensor(out=res[:, cols], in0=st[("gated", i)][:, cols], in1=x_sb[i][:, cols], op=ALU.add)
+                nc.vector.tensor_tensor(out=res[:, cols], in0=res[:, cols], in1=x_sb[i][:, cols], op=ALU.add)
                 nc.sync.dma_start(out=out_0[P * i : P * (i + 1), cols], in_=res[:, cols])
-            st[("result", i)] = res
 
         def round_result(i, groups=(0, GROUPS)):
             if ("rounded", i) not in st:
-                st[("rounded", i)] = two.tile([P, D], BF16, name="rounded")
+                st[("rounded", i)] = three.tile([P, D], BF16, name="rounded")
             g0, g1 = groups
             nc.scalar.copy(
                 out=st[("rounded", i)][:].rearrange("p (u m e) -> p u m e", u=2, e=2)[:, :, P * g0 : P * g1],
@@ -259,6 +258,21 @@ def tile_diffusionforcingpertokenadalnzero_x2_kernel(
                     in_=out_scales[32 * q : 32 * q + 4, :, P * i0 : P * i1].bitcast(I32),
                 )
 
+        def scale_mm(i):
+            product(("S", i), "wsc", st[("cgq", i)], ("sg0", "sg1"))
+
+        def shift_mm(i):
+            product(("H", i), "wsh", st[("cgq", i)], ("h0", "h1"))
+
+        def gate_mm(i):
+            product(("G", i), "wg", st[("cgq", i)], ("sg0", "sg1"))
+
+        def f_mm(i):
+            product(("F", i), "w", st[("ygq", i)], ("f0", "f1"))
+
+        def turn_result(i, tag="turn_o"):
+            turn_sorted(("oT", i), tag, st[("rounded", i)])
+
         turn_c(0)
         unload_turned(("cT", 0), "cg")
         for h in range(2):
@@ -267,65 +281,94 @@ def tile_diffusionforcingpertokenadalnzero_x2_kernel(
             nc.vector.tensor_copy(out=bias_all[:, HALF * h : HALF * (h + 1)], in_=b[:])
             if h == 0:
                 quantise(("cT", 0), "cg", four)
-        product(("S", 0), "wsc", st[("cgq", 0)], ("sg0", "sg1"))
+        scale_mm(0)
         row_mean(0)
         turn_c(1)
         unload_turned(("cT", 1), "cg")
+        row_squares(0)
+        add_bias(0)
+        quantise(("cT", 1), "cg", four)
+        row_std(0)
+        row_mean(1)
+        centre_times_gain(0)
         row_rstd(0)
+        shift_mm(0)
+        scale_mm(1)
+        row_squares(1)
+        row_std(1)
 
         last = TILES - 1
-        for j in range(TILES + 1):
-            now, before = j <= last, 1 <= j
+        for j in range(last):
             if j >= 2:
+                gate_times_f(j - 2)
+            make_y(j)
+            add_bias(j + 1)
+            turn_y(j)
+            if j + 2 <= last:
+                turn_c(j + 2)
+            if j >= 3:
+                turn_result(j - 3)
+            unload_turned(("yT", j), "yg")
+            if j + 2 <= last:
+                unload_turned(("cT", j + 2), "cg")
+            if j >= 3:
+                unload_turned(("oT", j - 3), "og")
+            if j >= 2:
+                add_residual(j - 2)
                 round_result(j - 2)
-            if now:
-                product(("H", j), "wsh", st[("cgq", j)], ("h0", "h1"))
-                add_bias(j)
-            if j + 1 <= last:
-                row_mean(j + 1)
-                quantise(("cT", j + 1), "cg", four)
-            if before:
-                product(("G", j - 1), "wg", st[("cgq", j - 1)], ("sg0", "sg1"))
-            if now:
-                centre_times_gain(j)
-            if before:
-                product(("F", j - 1), "w", st[("ygq", j - 1)], ("f0", "f1"))
-                unload_gate(j - 1)
+            row_rstd(j + 1)
+            if j + 2 <= last:
+                quantise(("cT", j + 2), "cg", four)
+            centre_times_gain(j + 1)
+            quantise(("yT", j), "yg", three)
             if j >= 3:
                 quantise_result(j - 3)
                 if j % 2 == 0:
                     store_words(j - 4, j - 2)
-            if now:
-                make_y(j)
-            if j + 1 <= last:
-                row_rstd(j + 1)
+            if j >= 1:
+                gate_mm(j - 1)
+                unload_gate(j - 1)
+                f_mm(j - 1)
+            shift_mm(j + 1)
             if j + 2 <= last:
-                turn_c(j + 2)
-            if now:
-                turn_sorted(("yT", j), "h0", st[("y", j)])
-            if j >= 2:
-                turn_sorted(("oT", j - 2), "turn_o", st[("rounded", j - 2)])
-            if now:
-                unload_turned(("yT", j), "yg")
-            if j + 2 <= last:
-                unload_turned(("cT", j + 2), "cg")
-            if j >= 2:
-                unload_turned(("oT", j - 2), "og")
-            if before:
-                gate_times_f(j - 1)
-            if now:
-                quantise(("yT", j), "yg", two)
-            if before:
-                add_residual(j - 1, 2 if j - 1 == last else 1)
-            if j + 1 <= last:
-                product(("S", j + 1), "wsc", st[("cgq", j + 1)], ("sg0", "sg1"))
+                scale_mm(j + 2)
+                row_mean(j + 2)
+                row_squares(j + 2)
+                row_std(j + 2)
 
-        quantise_result(last - 1)
-        store_words(last - 1, last)
-        store_scales(0, last, (nc.sync,))
+        gate_mm(6)
+        unload_gate(6)
+        gate_times_f(5)
+        make_y(7)
+        f_mm(6)
+        turn_y(7)
+        turn_result(4)
+        unload_turned(("yT", 7), "yg")
+        gate_mm(7)
+        add_residual(5)
+        round_result(5)
+        gate_times_f(6)
+        quantise(("yT", 7), "yg", three)
+        f_mm(7)
+        unload_gate(7)
+        turn_result(5, "turn_c")
+        add_residual(6)
+        unload_turned(("oT", 4), "og")
+        round_result(6)
+        gate_times_f(7)
+        quantise_result(4)
+        unload_turned(("oT", 5), "og")
+        turn_result(6)
+        add_residual(7, 2)
+        unload_turned(("oT", 6), "og")
+        quantise_result(5)
+        store_words(4, 6)
         for g in range(GROUPS):
             round_result(last, (g, g + 1))
-        turn_sorted(("oT", last), "turn_c", st[("rounded", last)])
+        quantise_result(6)
+        store_words(6, 7)
+        store_scales(0, last, (nc.sync,))
+        turn_result(last, "turn_c")
         for g in range(GROUPS):
             unload_turned(("oT", last), "og", (g, g + 1))
             quantise_result(last, (g, g + 1))

@@ -20,6 +20,7 @@ GROUPS = 2
 HALF = 512
 TILES = T // P
 EPS = 1e-6
+STATS_ON_VECTOR = (1,)
 
 
 def tile_diffusionforcingpertokenadalnzero_x2_kernel(
@@ -48,58 +49,54 @@ def tile_diffusionforcingpertokenadalnzero_x2_kernel(
         names = ("wsc", "wsh", "wg", "w")
         hbm_words = dict(zip(names, (wsc_words, wsh_words, wg_words, w_words)))
         hbm_scales = dict(zip(names, (wsc_scales, wsh_scales, wg_scales, w_scales)))
-        first_row = dict(zip(names, (0, 8, 0, 8)))
+        first_row = dict(zip(names, (0, 4, 8, 12)))
         words = {}
         scales = {}
         for n in names:
-            words[n] = [keep.tile([P, GROUPS, HALF], U32, name="%s_words%d" % (n, h), align_bytes=64) for h in range(2)]
-            scales[n] = keep.tile([P, D], U8, name="%s_scales" % n, align_bytes=64)
+            words[n] = keep.tile([P, GROUPS, D], U32, name="%s_words" % n, align_bytes=64)
+            scales[n] = keep.tile([P, GROUPS, D], U8, name="%s_scales" % n, align_bytes=64)
         out_words = keep.tile([P, GROUPS, T], U32, name="out_words", align_bytes=64)
         out_scales = keep.tile([P, GROUPS, T], U8, name="out_scales", align_bytes=64)
 
         def load_rows(dst, src, i):
             nc.sync.dma_start(out=dst[i][:], in_=src[P * i : P * (i + 1), :])
 
-        def load_scales(n):
+        def load_scales(n, engine):
             for q in range(4):
                 r = 32 * q + first_row[n]
-                nc.sync.dma_start(
-                    out=scales[n][:].bitcast(I32)[r : r + 8, :],
-                    in_=hbm_scales[n][:, 4 * q : 4 * q + 4, :].bitcast(I32),
+                engine.dma_start(
+                    out=scales[n][:].bitcast(I32)[r : r + 4],
+                    in_=hbm_scales[n][:, 4 * q : 4 * q + 4, :].rearrange("g r n -> r g n").bitcast(I32),
                 )
 
-        def load_words(n, h):
-            src = hbm_words[n].rearrange("g p n t -> p g (n t)")[:, :, 4 * HALF * h : 4 * HALF * (h + 1)]
-            nc.sync.dma_start(out=words[n][h][:].bitcast(I32), in_=src.bitcast(I32))
+        def load_words(n):
+            src = hbm_words[n].rearrange("g p n t -> p g (n t)")
+            nc.sync.dma_start(out=words[n][:].bitcast(I32), in_=src.bitcast(I32))
 
-        nc.vector.memset(bias_row[:], 0.0)
+        make_identity(nc, ident[:])
         nc.vector.memset(scales["wsc"][:].bitcast(I32), 0)
+        nc.vector.memset(bias_row[:], 0.0)
         nc.vector.memset(ones[:], 1.0)
         for n in names[1:]:
             nc.vector.memset(scales[n][:].bitcast(I32), 0)
-        make_identity(nc, ident[:])
         nc.scalar.activation(out=warm[:], in_=ones[:, 0:1], func=ACT.Sqrt)
 
+        for n in names[2:]:
+            load_scales(n, nc.gpsimd)
         load_rows(c_sb, c, 0)
+        load_scales("wsc", nc.sync)
         nc.sync.dma_start(out=bias_row[0:1, :], in_=bsc.rearrange("(o n) -> o n", o=1))
-        load_scales("wsc")
-        load_words("wsc", 0)
+        load_words("wsc")
         load_rows(x_sb, x, 0)
-        load_words("wsc", 1)
         load_rows(c_sb, c, 1)
-        load_scales("wsh")
-        load_words("wsh", 0)
-        load_words("wsh", 1)
+        load_scales("wsh", nc.sync)
+        load_words("wsh")
         load_rows(x_sb, x, 1)
         load_rows(c_sb, c, 2)
         load_rows(x_sb, x, 2)
         load_rows(c_sb, c, 3)
-        load_scales("wg")
-        load_words("wg", 0)
-        load_words("wg", 1)
-        load_scales("w")
-        load_words("w", 0)
-        load_words("w", 1)
+        load_words("wg")
+        load_words("w")
         for i in range(4, TILES + 1):
             load_rows(x_sb, x, i - 1)
             if i < TILES:
@@ -107,9 +104,9 @@ def tile_diffusionforcingpertokenadalnzero_x2_kernel(
 
         st = {}
 
-        def turn(key, tag, src_words):
+        def turn(key, tag, src_words, groups=(0, GROUPS)):
             b = bank(tag)
-            for g in range(GROUPS):
+            for g in range(*groups):
                 for u in range(2):
                     j = 2 * g + u
                     nc.tensor.transpose(b[:, P * j : P * (j + 1)], src_words(g, u), ident[:])
@@ -119,13 +116,13 @@ def tile_diffusionforcingpertokenadalnzero_x2_kernel(
             wv = c_sb[i][:].bitcast(F32)
             turn(("cT", i), "turn_c", lambda g, u: wv[:, 256 * g + u : 256 * (g + 1) : 2])
 
-        def turn_sorted(key, tag, tile):
+        def turn_sorted(key, tag, tile, groups):
             wv = tile[:].bitcast(F32)
-            turn(key, tag, lambda g, u: wv[:, 256 * u + P * g : 256 * u + P * (g + 1)])
+            turn(key, tag, lambda g, u: wv[:, 256 * u + P * g : 256 * u + P * (g + 1)], groups)
 
         def unload_turned(key, name, groups=(0, GROUPS)):
             if (name, key) not in st:
-                st[(name, key)] = three.tile([P, GROUPS, P, 4], BF16, name=name, align_bytes=64)
+                st[(name, key)] = four.tile([P, GROUPS, P, 4], BF16, name=name, align_bytes=64)
             dst = st[(name, key)]
             g0, g1 = groups
             nc.scalar.copy(
@@ -148,13 +145,12 @@ def tile_diffusionforcingpertokenadalnzero_x2_kernel(
             for h in range(2):
                 b = bank(tags[h])
                 for g in range(GROUPS):
-                    k = first_row[n] + 4 * g
                     nc.tensor.matmul_mx(
                         out=b[:],
                         lhsT=codes[:, P * g : P * (g + 1)].bitcast(FP8X4),
                         lhsT_scale=plane[:, P * g : P * (g + 1)],
-                        rhs=words[n][h][:, g, :].bitcast(FP8X4),
-                        rhs_scale=scales[n][k:P, HALF * h : HALF * (h + 1)],
+                        rhs=words[n][:, g, HALF * h : HALF * (h + 1)].bitcast(FP8X4),
+                        rhs_scale=scales[n][first_row[n] : P, g, HALF * h : HALF * (h + 1)],
                         start=(g == 0),
                         stop=(g == GROUPS - 1),
                     )
@@ -162,21 +158,39 @@ def tile_diffusionforcingpertokenadalnzero_x2_kernel(
             st[key] = banks
 
         def row_mean(i):
+            if i in STATS_ON_VECTOR:
+                return
             stats = keep.tile([P, 8], F32, name="stats%d" % i)
             junk = two.tile([P, D], BF16, name="junk")
             nc.scalar.activation(out=junk[:], in_=x_sb[i][:], func=ACT.Copy, scale=-1.0 / D, accum_out=stats[:, 0:1])
             st[("stats", i)] = stats
 
         def row_squares(i):
+            if i in STATS_ON_VECTOR:
+                return
             stats = st[("stats", i)]
             junk = two.tile([P, D], BF16, name="junk")
             nc.scalar.activation(
                 out=junk[:], in_=x_sb[i][:], func=ACT.Square, bias=stats[:, 0:1], accum_out=stats[:, 1:2]
             )
 
+        def row_partial_stats(i):
+            if i in STATS_ON_VECTOR:
+                parts = keep.tile([P, 2, 6], F32, name="parts%d" % i)
+                for h in range(2):
+                    nc.vector.bn_stats(out=parts[:, h], in_=x_sb[i][:, HALF * h : HALF * (h + 1)])
+                st[("parts", i)] = parts
+
+        def row_mean_var(i):
+            if i in STATS_ON_VECTOR:
+                stats = keep.tile([P, 8], F32, name="stats%d" % i)
+                nc.vector.bn_aggr(out=stats[:, 0:2], in_=st[("parts", i)][:].rearrange("p h s -> p (h s)"))
+                st[("stats", i)] = stats
+
         def row_std(i):
             stats = st[("stats", i)]
-            nc.scalar.activation(out=stats[:, 2:3], in_=stats[:, 1:2], func=ACT.Sqrt, scale=1.0 / D, bias=EPS)
+            scale = 1.0 if i in STATS_ON_VECTOR else 1.0 / D
+            nc.scalar.activation(out=stats[:, 2:3], in_=stats[:, 1:2], func=ACT.Sqrt, scale=scale, bias=EPS)
 
         def row_rstd(i):
             rstd = keep.tile([P, 1], F32, name="rstd%d" % i)
@@ -193,22 +207,25 @@ def tile_diffusionforcingpertokenadalnzero_x2_kernel(
         def centre_times_gain(i):
             a = st[("gain", i)]
             nc.vector.scalar_tensor_tensor(
-                out=a[:], in0=x_sb[i][:], scalar=st[("stats", i)][:, 0:1], in1=a[:], op0=ALU.add, op1=ALU.mult
+                out=a[:], in0=x_sb[i][:], scalar=st[("stats", i)][:, 0:1], in1=a[:],
+                op0=ALU.subtract if i in STATS_ON_VECTOR else ALU.add, op1=ALU.mult,
             )
 
         def make_y(i):
             y = three.tile([P, D], BF16, name="y")
-            for h in range(2):
-                cols = slice(HALF * h, HALF * (h + 1))
-                nc.vector.scalar_tensor_tensor(
-                    out=y[:, cols], in0=st[("gain", i)][:, cols], scalar=st[("rstd", i)][:], in1=st[("H", i)][h][:],
-                    op0=ALU.mult, op1=ALU.add,
-                )
+            yv = y[:].rearrange("p (u g m e) -> p g u m e", u=2, g=GROUPS, e=2)
+            tv = st[("gain", i)][:].rearrange("p (g m u e) -> p g u m e", g=GROUPS, u=2, e=2)
+            for g in range(GROUPS):
+                hv = st[("H", i)][g][:].rearrange("p (m u e) -> p u m e", u=2, e=2)
+                for u in range(2):
+                    nc.vector.scalar_tensor_tensor(
+                        out=yv[:, g, u], in0=tv[:, g, u], scalar=st[("rstd", i)][:], in1=hv[:, u],
+                        op0=ALU.mult, op1=ALU.add,
+                    )
             st[("y", i)] = y
 
         def turn_y(i):
-            wv = st[("y", i)][:].bitcast(F32)
-            turn(("yT", i), "h0", lambda g, u: wv[:, 256 * g + u : 256 * (g + 1) : 2])
+            turn_sorted(("yT", i), "h0", st[("y", i)], (0, GROUPS))
 
         def unload_gate(i):
             res = four.tile([P, D], F32, name="result")
@@ -222,18 +239,21 @@ def tile_diffusionforcingpertokenadalnzero_x2_kernel(
                 cols = slice(HALF * h, HALF * (h + 1))
                 nc.vector.tensor_tensor(out=res[:, cols], in0=st[("F", i)][h][:], in1=res[:, cols], op=ALU.mult)
 
-        def add_residual(i, parts=1):
+        def add_residual(i, engine, parts, stores):
             res = st[("result", i)]
             for h in range(parts):
                 cols = slice(D // parts * h, D // parts * (h + 1))
-                nc.vector.tensor_tensor(out=res[:, cols], in0=res[:, cols], in1=x_sb[i][:, cols], op=ALU.add)
-                nc.sync.dma_start(out=out_0[P * i : P * (i + 1), cols], in_=res[:, cols])
+                engine.tensor_tensor(out=res[:, cols], in0=res[:, cols], in1=x_sb[i][:, cols], op=ALU.add)
+                if stores == parts:
+                    nc.sync.dma_start(out=out_0[P * i : P * (i + 1), cols], in_=res[:, cols])
+            if stores != parts:
+                nc.sync.dma_start(out=out_0[P * i : P * (i + 1), :], in_=res[:])
 
-        def round_result(i, groups=(0, GROUPS)):
+        def round_result(i, copy, groups=(0, GROUPS)):
             if ("rounded", i) not in st:
                 st[("rounded", i)] = three.tile([P, D], BF16, name="rounded")
             g0, g1 = groups
-            nc.scalar.copy(
+            copy(
                 out=st[("rounded", i)][:].rearrange("p (u m e) -> p u m e", u=2, e=2)[:, :, P * g0 : P * g1],
                 in_=st[("result", i)][:].rearrange("p (m u e) -> p u m e", u=2, e=2)[:, :, P * g0 : P * g1],
             )
@@ -270,107 +290,115 @@ def tile_diffusionforcingpertokenadalnzero_x2_kernel(
         def f_mm(i):
             product(("F", i), "w", st[("ygq", i)], ("f0", "f1"))
 
-        def turn_result(i, tag="turn_o"):
-            turn_sorted(("oT", i), tag, st[("rounded", i)])
+        def turn_result(i, tag="turn_o", groups=(0, GROUPS)):
+            turn_sorted(("oT", i), tag, st[("rounded", i)], groups)
 
         turn_c(0)
         unload_turned(("cT", 0), "cg")
+        quantise(("cT", 0), "cg", four)
         for h in range(2):
             b = bank("f%d" % h)
             nc.tensor.matmul(out=b[:], lhsT=ones[:], rhs=bias_row[:, HALF * h : HALF * (h + 1)], start=True, stop=True)
-            nc.vector.tensor_copy(out=bias_all[:, HALF * h : HALF * (h + 1)], in_=b[:])
-            if h == 0:
-                quantise(("cT", 0), "cg", four)
+            nc.scalar.copy(out=bias_all[:, HALF * h : HALF * (h + 1)], in_=b[:])
         scale_mm(0)
         row_mean(0)
         turn_c(1)
-        unload_turned(("cT", 1), "cg")
         row_squares(0)
+        unload_turned(("cT", 1), "cg")
         add_bias(0)
+        centre_times_gain(0)
         quantise(("cT", 1), "cg", four)
         row_std(0)
-        row_mean(1)
-        centre_times_gain(0)
         row_rstd(0)
+        row_mean(1)
         shift_mm(0)
         scale_mm(1)
         row_squares(1)
-        row_std(1)
+        row_mean(2)
 
         last = TILES - 1
         for j in range(last):
             if j >= 2:
                 gate_times_f(j - 2)
+                add_residual(j - 2, nc.gpsimd, 2, 1)
             make_y(j)
+            if j == 0:
+                row_partial_stats(1)
             add_bias(j + 1)
+            if j == 0:
+                row_mean_var(1)
+            if j + 2 <= last:
+                row_partial_stats(j + 2)
             turn_y(j)
             if j + 2 <= last:
                 turn_c(j + 2)
             if j >= 3:
                 turn_result(j - 3)
             unload_turned(("yT", j), "yg")
+            row_std(j + 1)
             if j + 2 <= last:
                 unload_turned(("cT", j + 2), "cg")
             if j >= 3:
                 unload_turned(("oT", j - 3), "og")
-            if j >= 2:
-                add_residual(j - 2)
-                round_result(j - 2)
-            row_rstd(j + 1)
+            quantise(("yT", j), "yg", three)
+            if j + 2 <= last:
+                row_mean_var(j + 2)
+            centre_times_gain(j + 1)
             if j + 2 <= last:
                 quantise(("cT", j + 2), "cg", four)
-            centre_times_gain(j + 1)
-            quantise(("yT", j), "yg", three)
+            row_rstd(j + 1)
             if j >= 3:
                 quantise_result(j - 3)
                 if j % 2 == 0:
                     store_words(j - 4, j - 2)
+                if j == last - 1:
+                    store_scales(0, 4, (nc.sync,))
             if j >= 1:
                 gate_mm(j - 1)
                 unload_gate(j - 1)
                 f_mm(j - 1)
+            if j >= 2:
+                round_result(j - 2, nc.scalar.copy)
             shift_mm(j + 1)
             if j + 2 <= last:
                 scale_mm(j + 2)
-                row_mean(j + 2)
                 row_squares(j + 2)
-                row_std(j + 2)
+            if j + 3 <= last:
+                row_mean(j + 3)
 
         gate_mm(6)
         unload_gate(6)
         gate_times_f(5)
+        add_residual(5, nc.gpsimd, 2, 1)
         make_y(7)
-        f_mm(6)
         turn_y(7)
         turn_result(4)
+        f_mm(6)
         unload_turned(("yT", 7), "yg")
         gate_mm(7)
-        add_residual(5)
-        round_result(5)
-        gate_times_f(6)
         quantise(("yT", 7), "yg", three)
-        f_mm(7)
-        unload_gate(7)
-        turn_result(5, "turn_c")
-        add_residual(6)
+        gate_times_f(6)
         unload_turned(("oT", 4), "og")
-        round_result(6)
-        gate_times_f(7)
+        unload_gate(7)
+        f_mm(7)
+        round_result(5, nc.scalar.copy)
+        turn_result(5, "turn_c")
+        add_residual(6, nc.vector, 1, 1)
         quantise_result(4)
+        round_result(6, nc.vector.tensor_copy)
         unload_turned(("oT", 5), "og")
         turn_result(6)
-        add_residual(7, 2)
+        gate_times_f(7)
         unload_turned(("oT", 6), "og")
+        add_residual(7, nc.vector, 2, 2)
+        for g in range(GROUPS):
+            round_result(last, nc.scalar.copy, (g, g + 1))
         quantise_result(5)
-        store_words(4, 6)
-        for g in range(GROUPS):
-            round_result(last, (g, g + 1))
         quantise_result(6)
-        store_words(6, 7)
-        store_scales(0, last, (nc.sync,))
-        turn_result(last, "turn_c")
+        store_words(4, 7)
         for g in range(GROUPS):
+            turn_result(last, ("turn_c", "h1")[g], (g, g + 1))
             unload_turned(("oT", last), "og", (g, g + 1))
             quantise_result(last, (g, g + 1))
         store_words(last, TILES)
-        store_scales(last, TILES, (nc.scalar, nc.sync))
+        store_scales(4, TILES, (nc.scalar, nc.sync))

@@ -20,7 +20,16 @@ GROUPS = 2
 HALF = 512
 TILES = T // P
 EPS = 1e-6
-STATS_ON_VECTOR = (1,)
+STATS_ON_VECTOR = (0,)
+ADD_ON_VECTOR = (6, 7)
+ROUND_ON_VECTOR = (0, 1, 2, 7)
+ROUND_SHARED = ()
+STORE_AFTER = {1: 0, 3: 2, 5: 4, 7: 6}
+GATE_BANKS = ("sg0", "sg1")
+Y_BANK = "h0"
+LOADS = ("c0", "s:wsc", "bias", "x0", "w:wsc", "c1", "x1", "s:wsh", "w:wsh", "x2", "c2", "w:wg", "c3", "x3", "w:w", "c4", "x4", "c5", "x5", "c6", "x6", "c7", "x7")
+STEP = (("mean", 2), ("make_y", 0), ("scale_mm", 1), ("turn_out", -3), ("turn_y", 0), ("turn_c", 2), ("squares", 2), ("unload_out", -3), ("unload_y", 0), ("add_bias", 1), ("add_x", -2), ("std", 2), ("rstd", 1), ("unload_c", 2), ("round_out", -2), ("quantise_out", -5), ("f_mm", -1), ("centre", 1), ("gate_mm", 0), ("quantise_y", 0), ("shift_mm", 1), ("quantise_c", 2), ("mean_var", 3), ("gate_times_f", -1), ("spread_bias", 2), ("unload_gate", 0), ("partial_stats", 5))
+MOVED = {}
 
 
 def tile_diffusionforcingpertokenadalnzero_x2_kernel(
@@ -33,6 +42,7 @@ def tile_diffusionforcingpertokenadalnzero_x2_kernel(
         two = ctx.enter_context(tc.tile_pool(name="two", bufs=2))
         three = ctx.enter_context(tc.tile_pool(name="three", bufs=3))
         four = ctx.enter_context(tc.tile_pool(name="four", bufs=4))
+        five = ctx.enter_context(tc.tile_pool(name="five", bufs=5))
         psum = ctx.enter_context(tc.psum_pool(name="psum", bufs=1))
         ctx.enter_context(tc.manual_schedule())
 
@@ -83,24 +93,17 @@ def tile_diffusionforcingpertokenadalnzero_x2_kernel(
 
         for n in names[2:]:
             load_scales(n, nc.gpsimd)
-        load_rows(c_sb, c, 0)
-        load_scales("wsc", nc.sync)
-        nc.sync.dma_start(out=bias_row[0:1, :], in_=bsc.rearrange("(o n) -> o n", o=1))
-        load_words("wsc")
-        load_rows(x_sb, x, 0)
-        load_rows(c_sb, c, 1)
-        load_scales("wsh", nc.sync)
-        load_words("wsh")
-        load_rows(x_sb, x, 1)
-        load_rows(c_sb, c, 2)
-        load_rows(x_sb, x, 2)
-        load_rows(c_sb, c, 3)
-        load_words("wg")
-        load_words("w")
-        for i in range(4, TILES + 1):
-            load_rows(x_sb, x, i - 1)
-            if i < TILES:
-                load_rows(c_sb, c, i)
+        for item in LOADS:
+            if item == "bias":
+                nc.sync.dma_start(out=bias_row[0:1, :], in_=bsc.rearrange("(o n) -> o n", o=1))
+            elif item.startswith("s:"):
+                load_scales(item[2:], nc.sync)
+            elif item.startswith("w:"):
+                load_words(item[2:])
+            elif item.startswith("c"):
+                load_rows(c_sb, c, int(item[1:]))
+            else:
+                load_rows(x_sb, x, int(item[1:]))
 
         st = {}
 
@@ -198,7 +201,7 @@ def tile_diffusionforcingpertokenadalnzero_x2_kernel(
             st[("rstd", i)] = rstd
 
         def add_bias(i):
-            a = three.tile([P, D], F32, name="gain")
+            a = four.tile([P, D], F32, name="gain")
             for h in range(2):
                 cols = slice(HALF * h, HALF * (h + 1))
                 nc.vector.tensor_tensor(out=a[:, cols], in0=st[("S", i)][h][:], in1=bias_all[:, cols], op=ALU.add)
@@ -225,7 +228,7 @@ def tile_diffusionforcingpertokenadalnzero_x2_kernel(
             st[("y", i)] = y
 
         def turn_y(i):
-            turn_sorted(("yT", i), "h0", st[("y", i)], (0, GROUPS))
+            turn_sorted(("yT", i), Y_BANK, st[("y", i)], (0, GROUPS))
 
         def unload_gate(i):
             res = four.tile([P, D], F32, name="result")
@@ -285,120 +288,89 @@ def tile_diffusionforcingpertokenadalnzero_x2_kernel(
             product(("H", i), "wsh", st[("cgq", i)], ("h0", "h1"))
 
         def gate_mm(i):
-            product(("G", i), "wg", st[("cgq", i)], ("sg0", "sg1"))
+            product(("G", i), "wg", st[("cgq", i)], GATE_BANKS)
 
         def f_mm(i):
             product(("F", i), "w", st[("ygq", i)], ("f0", "f1"))
 
-        def turn_result(i, tag="turn_o", groups=(0, GROUPS)):
-            turn_sorted(("oT", i), tag, st[("rounded", i)], groups)
-
-        turn_c(0)
-        unload_turned(("cT", 0), "cg")
-        quantise(("cT", 0), "cg", four)
-        for h in range(2):
-            b = bank("f%d" % h)
-            nc.tensor.matmul(out=b[:], lhsT=ones[:], rhs=bias_row[:, HALF * h : HALF * (h + 1)], start=True, stop=True)
-            nc.scalar.copy(out=bias_all[:, HALF * h : HALF * (h + 1)], in_=b[:])
-        scale_mm(0)
-        row_mean(0)
-        turn_c(1)
-        row_squares(0)
-        unload_turned(("cT", 1), "cg")
-        add_bias(0)
-        centre_times_gain(0)
-        quantise(("cT", 1), "cg", four)
-        row_std(0)
-        row_rstd(0)
-        row_mean(1)
-        shift_mm(0)
-        scale_mm(1)
-        row_squares(1)
-        row_mean(2)
-
         last = TILES - 1
-        for j in range(last):
-            if j >= 2:
-                gate_times_f(j - 2)
-                add_residual(j - 2, nc.gpsimd, 2, 1)
-            make_y(j)
-            if j == 0:
-                row_partial_stats(1)
-            add_bias(j + 1)
-            if j == 0:
-                row_mean_var(1)
-            if j + 2 <= last:
-                row_partial_stats(j + 2)
-            turn_y(j)
-            if j + 2 <= last:
-                turn_c(j + 2)
-            if j >= 3:
-                turn_result(j - 3)
-            unload_turned(("yT", j), "yg")
-            row_std(j + 1)
-            if j + 2 <= last:
-                unload_turned(("cT", j + 2), "cg")
-            if j >= 3:
-                unload_turned(("oT", j - 3), "og")
-            quantise(("yT", j), "yg", three)
-            if j + 2 <= last:
-                row_mean_var(j + 2)
-            centre_times_gain(j + 1)
-            if j + 2 <= last:
-                quantise(("cT", j + 2), "cg", four)
-            row_rstd(j + 1)
-            if j >= 3:
-                quantise_result(j - 3)
-                if j % 2 == 0:
-                    store_words(j - 4, j - 2)
-                if j == last - 1:
-                    store_scales(0, 4, (nc.sync,))
-            if j >= 1:
-                gate_mm(j - 1)
-                unload_gate(j - 1)
-                f_mm(j - 1)
-            if j >= 2:
-                round_result(j - 2, nc.scalar.copy)
-            shift_mm(j + 1)
-            if j + 2 <= last:
-                scale_mm(j + 2)
-                row_squares(j + 2)
-            if j + 3 <= last:
-                row_mean(j + 3)
 
-        gate_mm(6)
-        unload_gate(6)
-        gate_times_f(5)
-        add_residual(5, nc.gpsimd, 2, 1)
-        make_y(7)
-        turn_y(7)
-        turn_result(4)
-        f_mm(6)
-        unload_turned(("yT", 7), "yg")
-        gate_mm(7)
-        quantise(("yT", 7), "yg", three)
-        gate_times_f(6)
-        unload_turned(("oT", 4), "og")
-        unload_gate(7)
-        f_mm(7)
-        round_result(5, nc.scalar.copy)
-        turn_result(5, "turn_c")
-        add_residual(6, nc.vector, 1, 1)
-        quantise_result(4)
-        round_result(6, nc.vector.tensor_copy)
-        unload_turned(("oT", 5), "og")
-        turn_result(6)
-        gate_times_f(7)
-        unload_turned(("oT", 6), "og")
-        add_residual(7, nc.vector, 2, 2)
-        for g in range(GROUPS):
-            round_result(last, nc.scalar.copy, (g, g + 1))
-        quantise_result(5)
-        quantise_result(6)
-        store_words(4, 7)
-        for g in range(GROUPS):
-            turn_result(last, ("turn_c", "h1")[g], (g, g + 1))
-            unload_turned(("oT", last), "og", (g, g + 1))
-            quantise_result(last, (g, g + 1))
-        store_words(last, TILES)
-        store_scales(4, TILES, (nc.scalar, nc.sync))
+        def halves(i):
+            return ((0, 1), (1, 2)) if i == last else ((0, GROUPS),)
+
+        def spread_bias(i):
+            if i == 0:
+                for h in range(2):
+                    b = bank("f%d" % h)
+                    cols = slice(HALF * h, HALF * (h + 1))
+                    nc.tensor.matmul(out=b[:], lhsT=ones[:], rhs=bias_row[:, cols], start=True, stop=True)
+                    nc.scalar.copy(out=bias_all[:, cols], in_=b[:])
+
+        def gpsimd_round(out, in_):
+            nc.gpsimd.tensor_scalar(out=out, in0=in_, scalar1=1.0, scalar2=-0.0, op0=ALU.mult, op1=ALU.add)
+
+        def add_x(i):
+            add_residual(i, nc.vector if i in ADD_ON_VECTOR else nc.gpsimd, 2, 2 if i == last else 1)
+            if i in ROUND_SHARED:
+                round_result(i, gpsimd_round, (0, 1))
+
+        def round_out(i):
+            if i in ROUND_SHARED:
+                round_result(i, nc.scalar.copy, (1, 2))
+                return
+            for groups in halves(i):
+                round_result(i, nc.vector.tensor_copy if i in ROUND_ON_VECTOR else nc.scalar.copy, groups)
+
+        def turn_out(i):
+            for groups, tag in zip(halves(i), ("turn_o", "turn_c")):
+                turn_sorted(("oT", i, groups), tag, st[("rounded", i)], groups)
+
+        def unload_out(i):
+            for groups in halves(i):
+                st[("oT", i)] = st[("oT", i, groups)]
+                unload_turned(("oT", i), "og", groups)
+
+        def quantise_out(i):
+            quantise_result(i)
+            if i in STORE_AFTER:
+                store_words(STORE_AFTER[i], i + 1)
+            if i == 3:
+                store_scales(0, 4, (nc.sync,))
+            if i == last:
+                store_scales(4, TILES, (nc.scalar, nc.sync))
+
+        tasks = {
+            "turn_c": turn_c,
+            "unload_c": lambda i: unload_turned(("cT", i), "cg"),
+            "quantise_c": lambda i: quantise(("cT", i), "cg", five),
+            "spread_bias": spread_bias,
+            "scale_mm": scale_mm,
+            "shift_mm": shift_mm,
+            "gate_mm": gate_mm,
+            "f_mm": f_mm,
+            "mean": row_mean,
+            "squares": row_squares,
+            "partial_stats": row_partial_stats,
+            "mean_var": row_mean_var,
+            "std": row_std,
+            "rstd": row_rstd,
+            "add_bias": add_bias,
+            "centre": centre_times_gain,
+            "make_y": make_y,
+            "turn_y": turn_y,
+            "unload_y": lambda i: unload_turned(("yT", i), "yg"),
+            "quantise_y": lambda i: quantise(("yT", i), "yg", three),
+            "unload_gate": unload_gate,
+            "gate_times_f": gate_times_f,
+            "add_x": add_x,
+            "round_out": round_out,
+            "turn_out": turn_out,
+            "unload_out": unload_out,
+            "quantise_out": quantise_out,
+        }
+        order = []
+        for i in range(TILES):
+            for place, (name, ahead) in enumerate(STEP):
+                order.append((MOVED.get((name, i), 32 * (i - ahead) + place), name, i))
+        for when, name, i in sorted(order):
+            tasks[name](i)

from contextlib import ExitStack

import concourse.mybir as mybir
from concourse.masks import make_identity

T, D = 1024, 1024
FLOPS = 4 * 2 * T * D * D

F32 = mybir.dt.float32
BF16 = mybir.dt.bfloat16
I32 = mybir.dt.int32
U32 = mybir.dt.uint32
U8 = mybir.dt.uint8
FP8X4 = mybir.dt.float8_e4m3fn_x4
ALU = mybir.AluOpType
ACT = mybir.ActivationFunctionType

P = 128
GROUPS = 2
HALF = 512
TILES = T // P
EPS = 1e-6
STATS_ON_VECTOR = (0,)
ADD_ON_VECTOR = (6, 7)
ROUND_ON_VECTOR = (0, 1, 2, 7)
ROUND_SHARED = ()
STORE_AFTER = {1: 0, 3: 2, 5: 4, 7: 6}
GATE_BANKS = ("sg0", "sg1")
Y_BANK = "h0"
LOADS = ("c0", "s:wsc", "bias", "x0", "w:wsc", "c1", "x1", "s:wsh", "w:wsh", "x2", "c2", "w:wg", "c3", "x3", "w:w", "c4", "x4", "c5", "x5", "c6", "x6", "c7", "x7")
STEP = (("mean", 2), ("make_y", 0), ("scale_mm", 1), ("turn_out", -3), ("turn_y", 0), ("turn_c", 2), ("squares", 2), ("unload_out", -3), ("unload_y", 0), ("add_bias", 1), ("add_x", -2), ("std", 2), ("rstd", 1), ("unload_c", 2), ("round_out", -2), ("quantise_out", -5), ("f_mm", -1), ("centre", 1), ("gate_mm", 0), ("quantise_y", 0), ("shift_mm", 1), ("quantise_c", 2), ("mean_var", 3), ("gate_times_f", -1), ("spread_bias", 2), ("unload_gate", 0), ("partial_stats", 5))
MOVED = {}


def tile_diffusionforcingpertokenadalnzero_x2_kernel(
    tc, x, c, wsc_words, wsc_scales, bsc, wsh_words, wsh_scales, wg_words, wg_scales, w_words, w_scales,
    out_0, out_1, out_2,
):
    nc = tc.nc
    with ExitStack() as ctx:
        keep = ctx.enter_context(tc.tile_pool(name="keep", bufs=1))
        two = ctx.enter_context(tc.tile_pool(name="two", bufs=2))
        three = ctx.enter_context(tc.tile_pool(name="three", bufs=3))
        four = ctx.enter_context(tc.tile_pool(name="four", bufs=4))
        five = ctx.enter_context(tc.tile_pool(name="five", bufs=5))
        psum = ctx.enter_context(tc.psum_pool(name="psum", bufs=1))
        ctx.enter_context(tc.manual_schedule())

        def bank(tag):
            return psum.tile([P, HALF], F32, name=tag)

        ident = keep.tile([P, P], F32, name="ident")
        ones = keep.tile([P, P], BF16, name="ones")
        bias_row = keep.tile([P, D], BF16, name="bias_row")
        bias_all = keep.tile([P, D], BF16, name="bias_all")
        warm = keep.tile([P, 1], F32, name="warm")
        x_sb = [keep.tile([P, D], BF16, name="x%d" % i) for i in range(TILES)]
        c_sb = [keep.tile([P, D], BF16, name="c%d" % i) for i in range(TILES)]
        names = ("wsc", "wsh", "wg", "w")
        hbm_words = dict(zip(names, (wsc_words, wsh_words, wg_words, w_words)))
        hbm_scales = dict(zip(names, (wsc_scales, wsh_scales, wg_scales, w_scales)))
        first_row = dict(zip(names, (0, 4, 8, 12)))
        words = {}
        scales = {}
        for n in names:
            words[n] = keep.tile([P, GROUPS, D], U32, name="%s_words" % n, align_bytes=64)
            scales[n] = keep.tile([P, GROUPS, D], U8, name="%s_scales" % n, align_bytes=64)
        out_words = keep.tile([P, GROUPS, T], U32, name="out_words", align_bytes=64)
        out_scales = keep.tile([P, GROUPS, T], U8, name="out_scales", align_bytes=64)

        def load_rows(dst, src, i):
            nc.sync.dma_start(out=dst[i][:], in_=src[P * i : P * (i + 1), :])

        def load_scales(n, engine):
            for q in range(4):
                r = 32 * q + first_row[n]
                engine.dma_start(
                    out=scales[n][:].bitcast(I32)[r : r + 4],
                    in_=hbm_scales[n][:, 4 * q : 4 * q + 4, :].rearrange("g r n -> r g n").bitcast(I32),
                )

        def load_words(n):
            src = hbm_words[n].rearrange("g p n t -> p g (n t)")
            nc.sync.dma_start(out=words[n][:].bitcast(I32), in_=src.bitcast(I32))

        make_identity(nc, ident[:])
        nc.vector.memset(scales["wsc"][:].bitcast(I32), 0)
        nc.vector.memset(bias_row[:], 0.0)
        nc.vector.memset(ones[:], 1.0)
        for n in names[1:]:
            nc.vector.memset(scales[n][:].bitcast(I32), 0)
        nc.scalar.activation(out=warm[:], in_=ones[:, 0:1], func=ACT.Sqrt)

        for n in names[2:]:
            load_scales(n, nc.gpsimd)
        for item in LOADS:
            if item == "bias":
                nc.sync.dma_start(out=bias_row[0:1, :], in_=bsc.rearrange("(o n) -> o n", o=1))
            elif item.startswith("s:"):
                load_scales(item[2:], nc.sync)
            elif item.startswith("w:"):
                load_words(item[2:])
            elif item.startswith("c"):
                load_rows(c_sb, c, int(item[1:]))
            else:
                load_rows(x_sb, x, int(item[1:]))

        st = {}

        def turn(key, tag, src_words, groups=(0, GROUPS)):
            b = bank(tag)
            for g in range(*groups):
                for u in range(2):
                    j = 2 * g + u
                    nc.tensor.transpose(b[:, P * j : P * (j + 1)], src_words(g, u), ident[:])
            st[key] = b

        def turn_c(i):
            wv = c_sb[i][:].bitcast(F32)
            turn(("cT", i), "turn_c", lambda g, u: wv[:, 256 * g + u : 256 * (g + 1) : 2])

        def turn_sorted(key, tag, tile, groups):
            wv = tile[:].bitcast(F32)
            turn(key, tag, lambda g, u: wv[:, 256 * u + P * g : 256 * u + P * (g + 1)], groups)

        def unload_turned(key, name, groups=(0, GROUPS)):
            if (name, key) not in st:
                st[(name, key)] = four.tile([P, GROUPS, P, 4], BF16, name=name, align_bytes=64)
            dst = st[(name, key)]
            g0, g1 = groups
            nc.scalar.copy(
                out=dst[:].rearrange("p g r t -> p (g r t)").bitcast(F32).rearrange("p (g r u) -> p g r u", g=GROUPS, u=2)[:, g0:g1],
                in_=st[key][:].rearrange("p (g u r) -> p g r u", g=GROUPS, u=2)[:, g0:g1],
            )

        def quantise(key, name, pool):
            src = st[(name, key)]
            codes = pool.tile([P, GROUPS * P], U32, name=name + "_codes", align_bytes=64)
            plane = pool.tile([P, GROUPS * P], U8, name=name + "_plane", align_bytes=64)
            nc.vector.quantize_mx(
                out=codes[:].bitcast(FP8X4), scales=plane[:], in_=src[:].rearrange("p g r t -> p (g r t)")
            )
            st[(name + "q", key[1])] = (codes, plane)

        def product(key, n, operand, tags):
            codes, plane = operand
            banks = []
            for h in range(2):
                b = bank(tags[h])
                for g in range(GROUPS):
                    nc.tensor.matmul_mx(
                        out=b[:],
                        lhsT=codes[:, P * g : P * (g + 1)].bitcast(FP8X4),
                        lhsT_scale=plane[:, P * g : P * (g + 1)],
                        rhs=words[n][:, g, HALF * h : HALF * (h + 1)].bitcast(FP8X4),
                        rhs_scale=scales[n][first_row[n] : P, g, HALF * h : HALF * (h + 1)],
                        start=(g == 0),
                        stop=(g == GROUPS - 1),
                    )
                banks.append(b)
            st[key] = banks

        def row_mean(i):
            if i in STATS_ON_VECTOR:
                return
            stats = keep.tile([P, 8], F32, name="stats%d" % i)
            junk = two.tile([P, D], BF16, name="junk")
            nc.scalar.activation(out=junk[:], in_=x_sb[i][:], func=ACT.Copy, scale=-1.0 / D, accum_out=stats[:, 0:1])
            st[("stats", i)] = stats

        def row_squares(i):
            if i in STATS_ON_VECTOR:
                return
            stats = st[("stats", i)]
            junk = two.tile([P, D], BF16, name="junk")
            nc.scalar.activation(
                out=junk[:], in_=x_sb[i][:], func=ACT.Square, bias=stats[:, 0:1], accum_out=stats[:, 1:2]
            )

        def row_partial_stats(i):
            if i in STATS_ON_VECTOR:
                parts = keep.tile([P, 2, 6], F32, name="parts%d" % i)
                for h in range(2):
                    nc.vector.bn_stats(out=parts[:, h], in_=x_sb[i][:, HALF * h : HALF * (h + 1)])
                st[("parts", i)] = parts

        def row_mean_var(i):
            if i in STATS_ON_VECTOR:
                stats = keep.tile([P, 8], F32, name="stats%d" % i)
                nc.vector.bn_aggr(out=stats[:, 0:2], in_=st[("parts", i)][:].rearrange("p h s -> p (h s)"))
                st[("stats", i)] = stats

        def row_std(i):
            stats = st[("stats", i)]
            scale = 1.0 if i in STATS_ON_VECTOR else 1.0 / D
            nc.scalar.activation(out=stats[:, 2:3], in_=stats[:, 1:2], func=ACT.Sqrt, scale=scale, bias=EPS)

        def row_rstd(i):
            rstd = keep.tile([P, 1], F32, name="rstd%d" % i)
            nc.vector.reciprocal(out=rstd[:], in_=st[("stats", i)][:, 2:3])
            st[("rstd", i)] = rstd

        def add_bias(i):
            a = four.tile([P, D], F32, name="gain")
            for h in range(2):
                cols = slice(HALF * h, HALF * (h + 1))
                nc.vector.tensor_tensor(out=a[:, cols], in0=st[("S", i)][h][:], in1=bias_all[:, cols], op=ALU.add)
            st[("gain", i)] = a

        def centre_times_gain(i):
            a = st[("gain", i)]
            nc.vector.scalar_tensor_tensor(
                out=a[:], in0=x_sb[i][:], scalar=st[("stats", i)][:, 0:1], in1=a[:],
                op0=ALU.subtract if i in STATS_ON_VECTOR else ALU.add, op1=ALU.mult,
            )

        def make_y(i):
            y = three.tile([P, D], BF16, name="y")
            yv = y[:].rearrange("p (u g m e) -> p g u m e", u=2, g=GROUPS, e=2)
            tv = st[("gain", i)][:].rearrange("p (g m u e) -> p g u m e", g=GROUPS, u=2, e=2)
            for g in range(GROUPS):
                hv = st[("H", i)][g][:].rearrange("p (m u e) -> p u m e", u=2, e=2)
                for u in range(2):
                    nc.vector.scalar_tensor_tensor(
                        out=yv[:, g, u], in0=tv[:, g, u], scalar=st[("rstd", i)][:], in1=hv[:, u],
                        op0=ALU.mult, op1=ALU.add,
                    )
            st[("y", i)] = y

        def turn_y(i):
            turn_sorted(("yT", i), Y_BANK, st[("y", i)], (0, GROUPS))

        def unload_gate(i):
            res = four.tile([P, D], F32, name="result")
            for h in range(2):
                nc.scalar.copy(out=res[:, HALF * h : HALF * (h + 1)], in_=st[("G", i)][h][:])
            st[("result", i)] = res

        def gate_times_f(i):
            res = st[("result", i)]
            for h in range(2):
                cols = slice(HALF * h, HALF * (h + 1))
                nc.vector.tensor_tensor(out=res[:, cols], in0=st[("F", i)][h][:], in1=res[:, cols], op=ALU.mult)

        def add_residual(i, engine, parts, stores):
            res = st[("result", i)]
            for h in range(parts):
                cols = slice(D // parts * h, D // parts * (h + 1))
                engine.tensor_tensor(out=res[:, cols], in0=res[:, cols], in1=x_sb[i][:, cols], op=ALU.add)
                if stores == parts:
                    nc.sync.dma_start(out=out_0[P * i : P * (i + 1), cols], in_=res[:, cols])
            if stores != parts:
                nc.sync.dma_start(out=out_0[P * i : P * (i + 1), :], in_=res[:])

        def round_result(i, copy, groups=(0, GROUPS)):
            if ("rounded", i) not in st:
                st[("rounded", i)] = three.tile([P, D], BF16, name="rounded")
            g0, g1 = groups
            copy(
                out=st[("rounded", i)][:].rearrange("p (u m e) -> p u m e", u=2, e=2)[:, :, P * g0 : P * g1],
                in_=st[("result", i)][:].rearrange("p (m u e) -> p u m e", u=2, e=2)[:, :, P * g0 : P * g1],
            )

        def quantise_result(i, groups=(0, GROUPS)):
            src = st[("og", ("oT", i))]
            cols = slice(P * i, P * (i + 1))
            for g in range(*groups):
                nc.vector.quantize_mx(
                    out=out_words[:, g, cols].bitcast(FP8X4), scales=out_scales[:, g, cols],
                    in_=src[:, g].rearrange("p r t -> p (r t)"),
                )

        def store_words(i0, i1):
            dst = out_1.rearrange("g p m t -> p g (m t)")[:, :, 4 * P * i0 : 4 * P * i1]
            nc.sync.dma_start(out=dst.bitcast(I32), in_=out_words[:, :, P * i0 : P * i1].bitcast(I32))

        def store_scales(i0, i1, engines):
            for q in range(4):
                engines[q % len(engines)].dma_start(
                    out=out_2[:, 4 * q : 4 * q + 4, P * i0 : P * i1].rearrange("g r m -> r g m").bitcast(I32),
                    in_=out_scales[32 * q : 32 * q + 4, :, P * i0 : P * i1].bitcast(I32),
                )

        def scale_mm(i):
            product(("S", i), "wsc", st[("cgq", i)], ("sg0", "sg1"))

        def shift_mm(i):
            product(("H", i), "wsh", st[("cgq", i)], ("h0", "h1"))

        def gate_mm(i):
            product(("G", i), "wg", st[("cgq", i)], GATE_BANKS)

        def f_mm(i):
            product(("F", i), "w", st[("ygq", i)], ("f0", "f1"))

        last = TILES - 1

        def halves(i):
            return ((0, 1), (1, 2)) if i == last else ((0, GROUPS),)

        def spread_bias(i):
            if i == 0:
                for h in range(2):
                    b = bank("f%d" % h)
                    cols = slice(HALF * h, HALF * (h + 1))
                    nc.tensor.matmul(out=b[:], lhsT=ones[:], rhs=bias_row[:, cols], start=True, stop=True)
                    nc.scalar.copy(out=bias_all[:, cols], in_=b[:])

        def gpsimd_round(out, in_):
            nc.gpsimd.tensor_scalar(out=out, in0=in_, scalar1=1.0, scalar2=-0.0, op0=ALU.mult, op1=ALU.add)

        def add_x(i):
            add_residual(i, nc.vector if i in ADD_ON_VECTOR else nc.gpsimd, 2, 2 if i == last else 1)
            if i in ROUND_SHARED:
                round_result(i, gpsimd_round, (0, 1))

        def round_out(i):
            if i in ROUND_SHARED:
                round_result(i, nc.scalar.copy, (1, 2))
                return
            for groups in halves(i):
                round_result(i, nc.vector.tensor_copy if i in ROUND_ON_VECTOR else nc.scalar.copy, groups)

        def turn_out(i):
            for groups, tag in zip(halves(i), ("turn_o", "turn_c")):
                turn_sorted(("oT", i, groups), tag, st[("rounded", i)], groups)

        def unload_out(i):
            for groups in halves(i):
                st[("oT", i)] = st[("oT", i, groups)]
                unload_turned(("oT", i), "og", groups)

        def quantise_out(i):
            quantise_result(i)
            if i in STORE_AFTER:
                store_words(STORE_AFTER[i], i + 1)
            if i == 3:
                store_scales(0, 4, (nc.sync,))
            if i == last:
                store_scales(4, TILES, (nc.scalar, nc.sync))

        tasks = {
            "turn_c": turn_c,
            "unload_c": lambda i: unload_turned(("cT", i), "cg"),
            "quantise_c": lambda i: quantise(("cT", i), "cg", five),
            "spread_bias": spread_bias,
            "scale_mm": scale_mm,
            "shift_mm": shift_mm,
            "gate_mm": gate_mm,
            "f_mm": f_mm,
            "mean": row_mean,
            "squares": row_squares,
            "partial_stats": row_partial_stats,
            "mean_var": row_mean_var,
            "std": row_std,
            "rstd": row_rstd,
            "add_bias": add_bias,
            "centre": centre_times_gain,
            "make_y": make_y,
            "turn_y": turn_y,
            "unload_y": lambda i: unload_turned(("yT", i), "yg"),
            "quantise_y": lambda i: quantise(("yT", i), "yg", three),
            "unload_gate": unload_gate,
            "gate_times_f": gate_times_f,
            "add_x": add_x,
            "round_out": round_out,
            "turn_out": turn_out,
            "unload_out": unload_out,
            "quantise_out": quantise_out,
        }
        order = []
        for i in range(TILES):
            for place, (name, ahead) in enumerate(STEP):
                order.append((MOVED.get((name, i), 32 * (i - ahead) + place), name, i))
        for when, name, i in sorted(order):
            tasks[name](i)
